import numpy as np
import ml_dtypes


def mxq(x, axis, fmt="e4m3"):
    dtype, down = {"e4m3": (ml_dtypes.float8_e4m3fn, 7), "e5m2": (ml_dtypes.float8_e5m2, 14)}[fmt]
    v = np.moveaxis(np.asarray(x, np.float32).astype(ml_dtypes.bfloat16).astype(np.float64), axis, -1)
    blocks = v.reshape(v.shape[:-1] + (-1, 32))
    amax = np.abs(blocks).max(-1, keepdims=True)
    byte = np.maximum(np.where(amax > 0, np.frexp(amax)[1] - 1 + 127, 0) - down, 1)
    scale = np.exp2(byte - 127.0)
    codes = (blocks / scale).astype(np.float32).astype(dtype).astype(np.float64)
    return np.moveaxis((codes * scale).reshape(v.shape), -1, axis)


WIDE = False


def mx_kscale(k):
    if not WIDE:
        return np.ones(k)
    levels = np.array([10, -10, 5, -5, 0])
    if k % 512:
        return np.exp2(np.random.permutation(np.resize(levels, k // 32))).repeat(32)
    a = np.empty((k // 512, 16))
    for p in range(k // 512):
        a[p, :8] = np.random.permutation(np.resize(levels, 8))
        for g in range(8):
            far = levels[np.abs(levels - a[p, g]) >= 10]
            a[p, g + 8] = far[np.random.randint(len(far))]
    return np.exp2(a.ravel()).repeat(32)


BF16 = ml_dtypes.bfloat16


def bf(x):
    return np.asarray(x, np.float32).astype(BF16)


def f64(x):
    return np.asarray(x).astype(np.float64)


E2M1 = np.array([0.0, 0.5, 1.0, 1.5, 2.0, 3.0, 4.0, 6.0, -0.0, -0.5, -1.0, -1.5, -2.0, -3.0, -4.0, -6.0])


def pack_weight(w, fmt):
    k, n = w.shape
    w = f64(bf(w)).reshape(k // 32, 32, n)
    amax = np.abs(w).max(1)
    if fmt == "e4m3":
        byte = np.frexp(amax)[1] - 1 + 127 - 7
    else:
        mant, ex = np.frexp(amax / 6.0)
        byte = np.where(mant > 0.5, ex, ex - 1) + 127
    byte = np.clip(np.where(amax > 0, byte, 1), 1, 254)
    scaled = (w * np.exp2(127.0 - byte)[:, None, :]).reshape(k, n).astype(np.float32)
    by_word = np.ascontiguousarray(scaled.reshape(k // 512, 128, 4, n).transpose(0, 1, 3, 2))
    if fmt == "e4m3":
        words = by_word.astype(ml_dtypes.float8_e4m3fn).view(np.uint8)
    else:
        c = by_word.astype(ml_dtypes.float4_e2m1fn).view(np.uint8) & 0xF
        words = c[..., 0::2] | (c[..., 1::2] << 4)
    return np.ascontiguousarray(words), np.ascontiguousarray(byte.astype(np.uint8).reshape(k // 512, 16, n))


def unpack_weight(words, scales, fmt):
    g, p, n, _ = words.shape
    if fmt == "e4m3":
        vals = np.ascontiguousarray(words).view(ml_dtypes.float8_e4m3fn).astype(np.float64)
    else:
        nib = np.empty((g, p, n, 4), np.uint8)
        nib[..., 0::2] = words & 0xF
        nib[..., 1::2] = words >> 4
        vals = E2M1[nib]
    vals = vals * np.repeat(np.exp2(scales.astype(np.float64) - 127.0), 8, axis=1)[..., None]
    return vals.transpose(0, 1, 3, 2).reshape(g * 512, n)

def planes(Y):
    n, m = Y.shape
    b = f64(bf(Y)).reshape(n // 32, 32, m)
    amax = np.abs(b).max(1)
    byte = np.clip(np.where(amax > 0, np.frexp(amax)[1] - 1 + 127 - 7, 1), 1, 254)
    codes = (b * np.exp2(127.0 - byte)[:, None, :]).reshape(n, m).astype(np.float32).astype(ml_dtypes.float8_e4m3fn).view(np.uint8)
    words = codes.reshape(n // 512, 128, 4, m).transpose(0, 1, 3, 2)
    return np.ascontiguousarray(words), np.ascontiguousarray(byte.astype(np.uint8).reshape(n // 512, 16, m))


F, C, T = 512, 1024, 1024


def setup_inputs():
    s = mx_kscale(C)
    t1, t2 = mx_kscale(T), mx_kscale(T)
    r = np.random.uniform(0.5, 1.5, (F, 1))
    a1 = np.random.uniform(0.5, 1.5, (C, 1))
    a2 = np.random.uniform(0.5, 1.5, (C, 1))
    w = np.random.standard_normal((F, C)) * r / np.sqrt(C) * s[None, :]
    w_words, w_scales = pack_weight(w.T, "e4m3")
    return {
        "w_words": w_words,
        "w_scales": w_scales,
        "x1": bf(np.random.standard_normal((C, T)) * a1 / s[:, None] * t1[None, :]),
        "x2": bf(np.random.standard_normal((C, T)) * a2 / s[:, None] * t2[None, :]),
        "tau1": bf(np.random.uniform(0.5, 1.5, T) / (t1 * t1)),
        "tau2": bf(np.random.uniform(0.5, 1.5, T) / (t2 * t2)),
        "p": bf(np.random.uniform(4.0, 12.0, C) * s),
    }


def _class_terms(wq, x, tau):
    z = wq @ mxq(x, 0, "e4m3")
    y = tau[None, :] * z
    v = np.mean(y * z, axis=1)
    m = mxq(y, 1, "e4m3") @ mxq(x, 1, "e4m3").T
    return m, v


def core(w_words, w_scales, x1, x2, tau1, tau2, p):
    n_t = x1.shape[1]
    wq = unpack_weight(w_words, w_scales, "e4m3").T
    m1, v1 = _class_terms(wq, f64(x1), f64(tau1))
    m2, v2 = _class_terms(wq, f64(x2), f64(tau2))
    g = (2.0 / n_t) * (m1 / v1[:, None] - m2 / v2[:, None])
    u = f64(p)[None, :] * g
    return u


def reference(w_words, w_scales, x1, x2, tau1, tau2, p):
    R_out = core(w_words, w_scales, x1, x2, tau1, tau2, p)
    words, scales = planes(R_out)
    return R_out, words, scales

@@ -1,0 +1,312 @@
+from contextlib import ExitStack
+
+import concourse.mybir as mybir
+from concourse.masks import make_identity
+
+F32 = mybir.dt.float32
+BF16 = mybir.dt.bfloat16
+U32 = mybir.dt.uint32
+I32 = mybir.dt.int32
+U8 = mybir.dt.uint8
+FP8X4 = mybir.dt.float8_e4m3fn_x4
+MUL = mybir.AluOpType.mult
+ADD = mybir.AluOpType.add
+COPY = mybir.ActivationFunctionType.Copy
+SQUARE = mybir.ActivationFunctionType.Square
+
+P = 128
+NF, NC, NT = 512, 1024, 1024
+FLOPS = 4 * 2 * NF * NC * NT
+
+SCALAR_A = ((0, 0, 1), (1, 0, 1))
+
+
+def tile_channelpreconditionedcsplogvarianceratio_x2_kernel(
+    tc, w_words, w_scales, x1, x2, tau1, tau2, p, out_0, out_1, out_2
+):
+    nc = tc.nc
+    with ExitStack() as ctx:
+        keep = ctx.enter_context(tc.tile_pool(name="keep", bufs=1))
+        work = ctx.enter_context(tc.tile_pool(name="work", bufs=4))
+        psum = ctx.enter_context(tc.psum_pool(name="psum", bufs=7))
+        vpool = ctx.enter_context(tc.psum_pool(name="vpool", bufs=1))
+        ctx.enter_context(tc.manual_schedule())
+
+        xs = {}
+        for k in range(2):
+            for g in range(2):
+                xs[k, g] = keep.tile([P, 4, NT], BF16, name="x_%d_%d" % (k, g), align_bytes=64)
+        x_hbm = [x.rearrange("(g p j) t -> g p j t", g=2, j=4) for x in (x1, x2)]
+
+        def load_x1(gt):
+            for g in range(2):
+                cols = slice(512 * gt, 512 * gt + 512)
+                nc.sync.dma_start(out=xs[0, g][:, :, cols], in_=x_hbm[0][g][:, :, cols])
+
+        load_x1(0)
+        w_sc = keep.tile([P, NF], U8, name="w_sc", align_bytes=64)
+        nc.vector.memset(w_sc[:].bitcast(I32), 0)
+        ident = keep.tile([P, P], F32, name="ident", align_bytes=64)
+        make_identity(nc, ident[:])
+        for q in range(4):
+            for g in range(2):
+                nc.sync.dma_start(
+                    out=w_sc[32 * q + 4 * g : 32 * q + 4 * g + 4, :].bitcast(I32),
+                    in_=w_scales[g][4 * q : 4 * q + 4, :].bitcast(I32),
+                )
+        tau = []
+        for k, t in enumerate((tau1, tau2)):
+            tau.append(keep.tile([P, 2, 4], BF16, name="tau_%d" % k, align_bytes=64))
+            nc.sync.dma_start(out=tau[k][:], in_=t.rearrange("(g p s) -> p g s", g=2, s=4))
+        w_sb = keep.tile([P, 2, NF], U32, name="w_sb", align_bytes=64)
+        for g in range(2):
+            nc.sync.dma_start(
+                out=w_sb[:, g, :].bitcast(I32), in_=w_words[g].rearrange("p n t -> p (n t)").bitcast(I32)
+            )
+        load_x1(1)
+        for g in range(2):
+            nc.sync.dma_start(out=xs[1, g][:], in_=x_hbm[1][g])
+        p_b = keep.tile([P, NC], BF16, name="p_b", align_bytes=64)
+        nc.sync.dma_start(out=p_b[:], in_=p.partition_broadcast(P))
+
+        half_tau = keep.tile([P, 2, 2, 4], F32, name="half_tau", align_bytes=64)
+
+        xc, xt, xtq, yg, yq, zsq, xg, vbank = {}, {}, {}, {}, {}, {}, {}, {}
+
+        def TR(k, g, gt):
+            xt[k, g, gt] = work.tile([P, 2048], BF16, name="xt", align_bytes=64)
+            banks = []
+            for jj in range(2):
+                bank = psum.tile([P, 2, 2, P], F32, name="bank")
+                banks.append(bank)
+                for u in range(2):
+                    for jl in range(2):
+                        words = xs[k, g][:, 2 * jj + jl, :].bitcast(F32)
+                        nc.tensor.transpose(
+                            bank[:, u, jl, :], words[:, 256 * gt + u : 256 * (gt + 1) : 2], ident[:]
+                        )
+            for jj in range(2):
+                dst = xt[k, g, gt][:].bitcast(F32).rearrange("p (q j u) -> p q j u", j=4, u=2)
+                nc.scalar.copy(
+                    out=dst[:, :, 2 * jj : 2 * jj + 2, :], in_=banks[jj][:].rearrange("p u j q -> p q j u")
+                )
+
+        def A(k, g, gt):
+            xg[k, g, gt] = work.tile([P, 2048], BF16, name="xg", align_bytes=64)
+            dst = xg[k, g, gt][:].rearrange("p (s m j) -> p s m j", s=4, j=4)
+            src = xs[k, g][:, :, 512 * gt : 512 * gt + 512].rearrange("p j (m s) -> p s m j", s=4)
+            if (k, g, gt) in SCALAR_A:
+                for s in range(4):
+                    nc.scalar.copy(out=dst[:, s], in_=src[:, s])
+            else:
+                nc.vector.tensor_copy(out=dst, in_=src)
+
+        def quant(src, name):
+            codes = keep.tile([P, 512], U32, name=name, align_bytes=64)
+            scales = keep.tile([P, 512], U8, name=name + "s", align_bytes=64)
+            nc.vector.quantize_mx(out=codes[:].bitcast(FP8X4), scales=scales[:], in_=src[:])
+            return codes, scales
+
+        def QC(k, g, gt):
+            xc[k, g, gt] = quant(xg[k, g, gt], "xc_%d%d%d" % (k, g, gt))
+
+        def QT(k, g, gt):
+            xtq[k, g, gt] = quant(xt[k, g, gt], "xq_%d%d%d" % (k, g, gt))
+
+        def QY(k, gt):
+            yq[k, gt] = quant(yg[k, gt], "yq_%d%d" % (k, gt))
+
+        def Z(k, gt, jf):
+            if (gt, jf) == (0, 0):
+                zsq[k] = work.tile([P, 2, 4, 4, P], F32, name="zsq", bufs=2, align_bytes=64)
+            if jf == 0:
+                yg[k, gt] = work.tile([P, 2048], BF16, name="yg", align_bytes=64)
+            z = psum.tile([P, 4, P], F32, name="z", tag="bank")
+            for s in range(4):
+                for g in range(2):
+                    codes, scales = xc[k, g, gt]
+                    nc.tensor.matmul_mx(
+                        out=z[:, s, :],
+                        lhsT=codes[:, 128 * s : 128 * s + 128].bitcast(FP8X4),
+                        lhsT_scale=scales[:, 128 * s : 128 * s + 128],
+                        rhs=w_sb[:, g, 128 * jf : 128 * jf + 128].bitcast(FP8X4),
+                        rhs_scale=w_sc[4 * g : P, 128 * jf : 128 * jf + 128],
+                        start=(g == 0),
+                        stop=(g == 1),
+                    )
+            dst = yg[k, gt][:].rearrange("p (t m s) -> p t m s", t=4, s=4)[:, :, 32 * jf : 32 * jf + 32, :]
+            nc.vector.tensor_tensor(
+                out=dst,
+                in0=z[:].rearrange("p s (m t) -> p t m s", t=4),
+                in1=tau[k][:, gt, :].unsqueeze(1).unsqueeze(1).to_broadcast([P, 4, 32, 4]),
+                op=MUL,
+            )
+            nc.scalar.activation(
+                out=zsq[k][:, gt, :, :, 32 * jf : 32 * jf + 32],
+                in_=z[:].rearrange("p s (m t) -> p t s m", t=4),
+                func=SQUARE,
+            )
+
+        def VAR(k, gt):
+            if gt == 0:
+                vbank[k] = vpool.tile([P, 2, 4], F32, name="v")
+            for t in range(4):
+                for s in range(4):
+                    nc.tensor.matmul(
+                        vbank[k][:, gt, t : t + 1],
+                        zsq[k][:, gt, t, s, :],
+                        half_tau[:, k, gt, s : s + 1],
+                        start=(s == 0),
+                        stop=(s == 3),
+                    )
+
+        def R(k):
+            v0 = keep.tile([P, 4], F32, name="v0_%d" % k)
+            nc.vector.tensor_copy(out=v0[:], in_=vbank[k][:, 0, :])
+            v = keep.tile([P, 4], F32, name="v_%d" % k)
+            nc.vector.tensor_tensor(out=v[:], in0=vbank[k][:, 1, :], in1=v0[:], op=ADD)
+            r = keep.tile([P, 4], F32, name="r_%d" % k)
+            nc.vector.reciprocal(out=r[:], in_=v[:])
+            return r
+
+        def stage2(k, t, c0, width, out):
+            for gt in range(2):
+                codes, scales = xtq[k, c0 // 512, gt]
+                cols = slice(c0 % 512, c0 % 512 + width)
+                nc.tensor.matmul_mx(
+                    out=out,
+                    lhsT=yq[k, gt][0][:, 128 * t : 128 * t + 128].bitcast(FP8X4),
+                    lhsT_scale=yq[k, gt][1][:, 128 * t : 128 * t + 128],
+                    rhs=codes[:, cols].bitcast(FP8X4),
+                    rhs_scale=scales[:, cols],
+                    start=(gt == 0),
+                    stop=(gt == 1),
+                )
+
+        a = keep.tile([P, 4, NC], F32, name="a", align_bytes=64)
+
+        def M0(h, r):
+            for t in range(4):
+                m = psum.tile([P, 512], F32, name="m", tag="bank")
+                stage2(0, t, 512 * h, 512, m[:])
+                nc.scalar.activation(out=a[:, t, 512 * h : 512 * h + 512], in_=m[:], func=COPY, scale=r[:, t : t + 1])
+
+        TR(0, 0, 0)
+        A(0, 0, 0)
+        TR(0, 1, 0)
+        A(0, 1, 0)
+        QC(0, 0, 0)
+        QC(0, 1, 0)
+        A(0, 0, 1)
+        nc.vector.tensor_scalar(out=half_tau[:, 0], in0=tau[0][:], scalar1=0.5, scalar2=None, op0=MUL)
+        nc.vector.tensor_scalar(out=half_tau[:, 1], in0=tau[1][:], scalar1=-0.5, scalar2=None, op0=MUL)
+        Z(0, 0, 0)
+        A(0, 1, 1)
+        Z(0, 0, 1)
+        Z(0, 0, 2)
+        Z(0, 0, 3)
+        QC(0, 0, 1)
+        QC(0, 1, 1)
+        TR(0, 0, 1)
+        TR(0, 1, 1)
+        QT(0, 0, 0)
+        QT(0, 1, 0)
+        QY(0, 0)
+        for jf in range(4):
+            Z(0, 1, jf)
+        VAR(0, 0)
+        A(1, 0, 1)
+        VAR(0, 1)
+        TR(1, 0, 0)
+        TR(1, 0, 1)
+        QT(0, 0, 1)
+        QT(0, 1, 1)
+        QY(0, 1)
+        A(1, 0, 0)
+        TR(1, 1, 0)
+        TR(1, 1, 1)
+        A(1, 1, 0)
+        r1 = R(0)
+        QC(1, 0, 0)
+        QC(1, 1, 0)
+        M0(0, r1)
+        A(1, 1, 1)
+        for jf in range(4):
+            Z(1, 0, jf)
+        M0(1, r1)
+        QC(1, 0, 1)
+        QC(1, 1, 1)
+        QT(1, 0, 0)
+        QT(1, 0, 1)
+        QY(1, 0)
+        for jf in range(4):
+            Z(1, 1, jf)
+        VAR(1, 0)
+        VAR(1, 1)
+        QY(1, 1)
+        QT(1, 1, 0)
+        QT(1, 1, 1)
+        r2 = R(1)
+
+        out_rows = out_0.rearrange("(p t) c -> p t c", t=4)
+        words_hbm = out_1[0].rearrange("p m t -> p (m t)").bitcast(I32)
+        o_codes = keep.tile([P, NC], U32, name="o_codes", align_bytes=64)
+        o_scales = keep.tile([P, NC], U8, name="o_scales", align_bytes=64)
+        pend = []
+        late = []
+
+        def finish(c0, width, o):
+            cols = slice(c0, c0 + width)
+            og = work.tile([P, 4 * width], BF16, name="og_%d" % c0, bufs=1, align_bytes=64)
+            nc.scalar.copy(out=og[:].rearrange("p (c t) -> p c t", t=4), in_=o[:].rearrange("p t c -> p c t"))
+            late.append((c0, cols, og))
+
+        def quant_out():
+            c0, cols, og = late.pop(0)
+            nc.vector.quantize_mx(out=o_codes[:, cols].bitcast(FP8X4), scales=o_scales[:, cols], in_=og[:])
+            nc.sync.dma_start(out=words_hbm[:, cols], in_=o_codes[:, cols].bitcast(I32))
+            if c0 == 256:
+                store_scales(0, 512)
+            if c0 == 768:
+                store_scales(512, 512)
+
+        def store_scales(c0, width):
+            cols = slice(c0, c0 + width)
+            for q in range(4):
+                (nc.sync if q % 2 == 0 else nc.scalar).dma_start(
+                    out=out_2[0][4 * q : 4 * q + 4, cols].bitcast(I32),
+                    in_=o_scales[32 * q : 32 * q + 4, cols].bitcast(I32),
+                )
+
+        for c0, width in ((0, 256), (256, 256), (512, 256), (768, 256)):
+            cols = slice(c0, c0 + width)
+            o = work.tile([P, 4, width], F32, name="o", align_bytes=64)
+            for tp in range(2):
+                m = psum.tile([P, 2, width], F32, name="m2", tag="bank")
+                u = work.tile([P, 2, width], F32, name="u", align_bytes=64)
+                for tl in range(2):
+                    stage2(1, 2 * tp + tl, c0, width, m[:, tl, :])
+                for tl in range(2):
+                    t = 2 * tp + tl
+                    nc.vector.scalar_tensor_tensor(
+                        out=u[:, tl, :], in0=m[:, tl, :], scalar=r2[:, t : t + 1], in1=a[:, t, cols], op0=MUL, op1=ADD
+                    )
+                pend.append((o, tp, u, cols, c0, width))
+                if len(pend) > 1:
+                    step(nc, pend.pop(0), p_b, out_rows, finish)
+                if tp == 1 and late:
+                    quant_out()
+        while pend:
+            step(nc, pend.pop(0), p_b, out_rows, finish)
+        while late:
+            quant_out()
+
+
+def step(nc, item, p_b, out_rows, finish):
+    o, tp, u, cols, c0, width = item
+    nc.vector.tensor_tensor(
+        out=o[:, 2 * tp : 2 * tp + 2, :], in0=u[:], in1=p_b[:, cols].unsqueeze(1).to_broadcast([P, 2, width]), op=MUL
+    )
+    nc.sync.dma_start(out=out_rows[:, 2 * tp : 2 * tp + 2, cols], in_=o[:, 2 * tp : 2 * tp + 2, :])
+    if tp == 1:
+        finish(c0, width, o)

@@ -19,6 +19,7 @@ NF, NC, NT = 512, 1024, 1024
 FLOPS = 4 * 2 * NF * NC * NT
 
 SCALAR_A = ((0, 0, 1), (1, 0, 1))
+GPSIMD_A = ((0, 1, 1), (1, 1, 1))
 
 
 def tile_channelpreconditionedcsplogvarianceratio_x2_kernel(
@@ -32,16 +33,14 @@ def tile_channelpreconditionedcsplogvarianceratio_x2_kernel(
         vpool = ctx.enter_context(tc.psum_pool(name="vpool", bufs=1))
         ctx.enter_context(tc.manual_schedule())
 
-        xs = {}
-        for k in range(2):
-            for g in range(2):
-                xs[k, g] = keep.tile([P, 4, NT], BF16, name="x_%d_%d" % (k, g), align_bytes=64)
         x_hbm = [x.rearrange("(g p j) t -> g p j t", g=2, j=4) for x in (x1, x2)]
+        xs = {}
 
         def load_x1(gt):
             for g in range(2):
-                cols = slice(512 * gt, 512 * gt + 512)
-                nc.sync.dma_start(out=xs[0, g][:, :, cols], in_=x_hbm[0][g][:, :, cols])
+                x_half = keep.tile([P, 4, 512], BF16, name="x_0_%d_%d" % (g, gt), align_bytes=64)
+                nc.sync.dma_start(out=x_half[:], in_=x_hbm[0][g][:, :, 512 * gt : 512 * gt + 512])
+                xs[0, g, gt] = x_half[:]
 
         load_x1(0)
         w_sc = keep.tile([P, NF], U8, name="w_sc", align_bytes=64)
@@ -49,23 +48,24 @@ def tile_channelpreconditionedcsplogvarianceratio_x2_kernel(
         ident = keep.tile([P, P], F32, name="ident", align_bytes=64)
         make_identity(nc, ident[:])
         for q in range(4):
-            for g in range(2):
-                nc.sync.dma_start(
-                    out=w_sc[32 * q + 4 * g : 32 * q + 4 * g + 4, :].bitcast(I32),
-                    in_=w_scales[g][4 * q : 4 * q + 4, :].bitcast(I32),
-                )
-        tau = []
-        for k, t in enumerate((tau1, tau2)):
-            tau.append(keep.tile([P, 2, 4], BF16, name="tau_%d" % k, align_bytes=64))
-            nc.sync.dma_start(out=tau[k][:], in_=t.rearrange("(g p s) -> p g s", g=2, s=4))
+            nc.sync.dma_start(
+                out=w_sc[32 * q : 32 * q + 8, :].bitcast(I32), in_=w_scales[:, 4 * q : 4 * q + 4, :].bitcast(I32)
+            )
         w_sb = keep.tile([P, 2, NF], U32, name="w_sb", align_bytes=64)
         for g in range(2):
             nc.sync.dma_start(
                 out=w_sb[:, g, :].bitcast(I32), in_=w_words[g].rearrange("p n t -> p (n t)").bitcast(I32)
             )
+        tau = []
+        for k, t in enumerate((tau1, tau2)):
+            tau.append(keep.tile([P, 2, 4], BF16, name="tau_%d" % k, align_bytes=64))
+            nc.sync.dma_start(out=tau[k][:], in_=t.rearrange("(g p s) -> p g s", g=2, s=4))
         load_x1(1)
         for g in range(2):
-            nc.sync.dma_start(out=xs[1, g][:], in_=x_hbm[1][g])
+            x_whole = keep.tile([P, 4, NT], BF16, name="x_1_%d" % g, align_bytes=64)
+            nc.sync.dma_start(out=x_whole[:], in_=x_hbm[1][g])
+            for gt in range(2):
+                xs[1, g, gt] = x_whole[:, :, 512 * gt : 512 * gt + 512]
         p_b = keep.tile([P, NC], BF16, name="p_b", align_bytes=64)
         nc.sync.dma_start(out=p_b[:], in_=p.partition_broadcast(P))
 
@@ -81,9 +81,9 @@ def tile_channelpreconditionedcsplogvarianceratio_x2_kernel(
                 banks.append(bank)
                 for u in range(2):
                     for jl in range(2):
-                        words = xs[k, g][:, 2 * jj + jl, :].bitcast(F32)
+                        words = xs[k, g, gt][:, 2 * jj + jl, :].bitcast(F32)
                         nc.tensor.transpose(
-                            bank[:, u, jl, :], words[:, 256 * gt + u : 256 * (gt + 1) : 2], ident[:]
+                            bank[:, u, jl, :], words[:, u:256:2], ident[:]
                         )
             for jj in range(2):
                 dst = xt[k, g, gt][:].bitcast(F32).rearrange("p (q j u) -> p q j u", j=4, u=2)
@@ -92,12 +92,17 @@ def tile_channelpreconditionedcsplogvarianceratio_x2_kernel(
                 )
 
         def A(k, g, gt):
-            xg[k, g, gt] = work.tile([P, 2048], BF16, name="xg", align_bytes=64)
+            xg[k, g, gt] = work.tile([P, 2048], BF16, name="xg", bufs=3, align_bytes=64)
             dst = xg[k, g, gt][:].rearrange("p (s m j) -> p s m j", s=4, j=4)
-            src = xs[k, g][:, :, 512 * gt : 512 * gt + 512].rearrange("p j (m s) -> p s m j", s=4)
+            src = xs[k, g, gt].rearrange("p j (m s) -> p s m j", s=4)
             if (k, g, gt) in SCALAR_A:
                 for s in range(4):
                     nc.scalar.copy(out=dst[:, s], in_=src[:, s])
+            elif (k, g, gt) in GPSIMD_A:
+                for s in range(4):
+                    nc.gpsimd.tensor_scalar(
+                        out=dst[:, s], in0=src[:, s], scalar1=1.0, scalar2=0.0, op0=MUL, op1=ADD
+                    )
             else:
                 nc.vector.tensor_copy(out=dst, in_=src)
 
@@ -147,24 +152,33 @@ def tile_channelpreconditionedcsplogvarianceratio_x2_kernel(
                 func=SQUARE,
             )
 
-        def VAR(k, gt):
-            if gt == 0:
-                vbank[k] = vpool.tile([P, 2, 4], F32, name="v")
+        def WT(k, gt, engine):
+            for s in range(4):
+                sq = zsq[k][:, gt, :, s, :]
+                weight = half_tau[:, k, gt, s : s + 1]
+                if engine == "VS" and s < 2:
+                    nc.scalar.activation(out=sq, in_=sq, func=COPY, scale=weight)
+                elif engine == "G":
+                    nc.gpsimd.tensor_scalar(out=sq, in0=sq, scalar1=weight, scalar2=0.0, op0=MUL, op1=ADD)
+                else:
+                    nc.vector.tensor_scalar(out=sq, in0=sq, scalar1=weight, scalar2=None, op0=MUL)
+
+        def VAR(k):
+            vbank[k] = vpool.tile([P, 4, P], F32, name="v")
             for t in range(4):
-                for s in range(4):
+                for i in range(8):
                     nc.tensor.matmul(
-                        vbank[k][:, gt, t : t + 1],
-                        zsq[k][:, gt, t, s, :],
-                        half_tau[:, k, gt, s : s + 1],
-                        start=(s == 0),
-                        stop=(s == 3),
+                        vbank[k][:, t, :],
+                        zsq[k][:, i // 4, t, i % 4, :],
+                        ident[:],
+                        is_transpose=True,
+                        start=(i == 0),
+                        stop=(i == 7),
                     )
 
         def R(k):
-            v0 = keep.tile([P, 4], F32, name="v0_%d" % k)
-            nc.vector.tensor_copy(out=v0[:], in_=vbank[k][:, 0, :])
             v = keep.tile([P, 4], F32, name="v_%d" % k)
-            nc.vector.tensor_tensor(out=v[:], in0=vbank[k][:, 1, :], in1=v0[:], op=ADD)
+            nc.vector.tensor_reduce(out=v[:], in_=vbank[k][:], op=ADD, axis=mybir.AxisListType.X)
             r = keep.tile([P, 4], F32, name="r_%d" % k)
             nc.vector.reciprocal(out=r[:], in_=v[:])
             return r
@@ -198,52 +212,52 @@ def tile_channelpreconditionedcsplogvarianceratio_x2_kernel(
         QC(0, 0, 0)
         QC(0, 1, 0)
         A(0, 0, 1)
+        A(0, 1, 1)
         nc.vector.tensor_scalar(out=half_tau[:, 0], in0=tau[0][:], scalar1=0.5, scalar2=None, op0=MUL)
         nc.vector.tensor_scalar(out=half_tau[:, 1], in0=tau[1][:], scalar1=-0.5, scalar2=None, op0=MUL)
-        Z(0, 0, 0)
-        A(0, 1, 1)
-        Z(0, 0, 1)
-        Z(0, 0, 2)
-        Z(0, 0, 3)
+        for jf in range(4):
+            Z(0, 0, jf)
+        WT(0, 0, "G")
         QC(0, 0, 1)
         QC(0, 1, 1)
+        QT(0, 0, 0)
+        QY(0, 0)
         TR(0, 0, 1)
         TR(0, 1, 1)
-        QT(0, 0, 0)
-        QT(0, 1, 0)
-        QY(0, 0)
         for jf in range(4):
             Z(0, 1, jf)
-        VAR(0, 0)
-        A(1, 0, 1)
-        VAR(0, 1)
+        QT(0, 1, 0)
+        QY(0, 1)
+        WT(0, 1, "V")
         TR(1, 0, 0)
         TR(1, 0, 1)
+        VAR(0)
         QT(0, 0, 1)
         QT(0, 1, 1)
-        QY(0, 1)
         A(1, 0, 0)
+        r1 = R(0)
+        A(1, 1, 0)
+        A(1, 0, 1)
+        M0(0, r1)
         TR(1, 1, 0)
         TR(1, 1, 1)
-        A(1, 1, 0)
-        r1 = R(0)
         QC(1, 0, 0)
         QC(1, 1, 0)
-        M0(0, r1)
         A(1, 1, 1)
+        QT(1, 0, 0)
         for jf in range(4):
             Z(1, 0, jf)
-        M0(1, r1)
         QC(1, 0, 1)
         QC(1, 1, 1)
-        QT(1, 0, 0)
-        QT(1, 0, 1)
         QY(1, 0)
         for jf in range(4):
             Z(1, 1, jf)
-        VAR(1, 0)
-        VAR(1, 1)
+        WT(1, 0, "G")
         QY(1, 1)
+        QT(1, 0, 1)
+        WT(1, 1, "VS")
+        M0(1, r1)
+        VAR(1)
         QT(1, 1, 0)
         QT(1, 1, 1)
         r2 = R(1)
@@ -252,23 +266,51 @@ def tile_channelpreconditionedcsplogvarianceratio_x2_kernel(
         words_hbm = out_1[0].rearrange("p m t -> p (m t)").bitcast(I32)
         o_codes = keep.tile([P, NC], U32, name="o_codes", align_bytes=64)
         o_scales = keep.tile([P, NC], U8, name="o_scales", align_bytes=64)
-        pend = []
-        late = []
+        chunks = [(256 * i, 256) for i in range(4)]
+        u_of, o_of, og_of = {}, {}, {}
 
-        def finish(c0, width, o):
+        def F2(i, tp):
+            c0, width = chunks[i]
+            m = psum.tile([P, 2, width], F32, name="m2", tag="bank")
+            for tl in range(2):
+                stage2(1, 2 * tp + tl, c0, width, m[:, tl, :])
+            u = work.tile([P, 2, width], F32, name="u", bufs=6, align_bytes=64)
+            for tl in range(2):
+                t = 2 * tp + tl
+                nc.vector.scalar_tensor_tensor(
+                    out=u[:, tl, :],
+                    in0=m[:, tl, :],
+                    scalar=r2[:, t : t + 1],
+                    in1=a[:, t, c0 : c0 + width],
+                    op0=MUL,
+                    op1=ADD,
+                )
+            u_of[i, tp] = u
+
+        def F3(i, tp, engine):
+            c0, width = chunks[i]
             cols = slice(c0, c0 + width)
-            og = work.tile([P, 4 * width], BF16, name="og_%d" % c0, bufs=1, align_bytes=64)
-            nc.scalar.copy(out=og[:].rearrange("p (c t) -> p c t", t=4), in_=o[:].rearrange("p t c -> p c t"))
-            late.append((c0, cols, og))
+            if i not in o_of:
+                o_of[i] = work.tile([P, 4, width], F32, name="o", align_bytes=64)
+            rows = slice(2 * tp, 2 * tp + 2)
+            engine.tensor_tensor(
+                out=o_of[i][:, rows, :],
+                in0=u_of[i, tp][:],
+                in1=p_b[:, cols].unsqueeze(1).to_broadcast([P, 2, width]),
+                op=MUL,
+            )
+            nc.sync.dma_start(out=out_rows[:, rows, cols], in_=o_of[i][:, rows, :])
 
-        def quant_out():
-            c0, cols, og = late.pop(0)
-            nc.vector.quantize_mx(out=o_codes[:, cols].bitcast(FP8X4), scales=o_scales[:, cols], in_=og[:])
+        def F4(i, copy):
+            width = chunks[i][1]
+            og_of[i] = work.tile([P, 4 * width], BF16, name="og", align_bytes=64)
+            copy(out=og_of[i][:].rearrange("p (c t) -> p c t", t=4), in_=o_of[i][:].rearrange("p t c -> p c t"))
+
+        def QO(i):
+            c0, width = chunks[i]
+            cols = slice(c0, c0 + width)
+            nc.vector.quantize_mx(out=o_codes[:, cols].bitcast(FP8X4), scales=o_scales[:, cols], in_=og_of[i][:])
             nc.sync.dma_start(out=words_hbm[:, cols], in_=o_codes[:, cols].bitcast(I32))
-            if c0 == 256:
-                store_scales(0, 512)
-            if c0 == 768:
-                store_scales(512, 512)
 
         def store_scales(c0, width):
             cols = slice(c0, c0 + width)
@@ -278,35 +320,22 @@ def tile_channelpreconditionedcsplogvarianceratio_x2_kernel(
                     in_=o_scales[32 * q : 32 * q + 4, cols].bitcast(I32),
                 )
 
-        for c0, width in ((0, 256), (256, 256), (512, 256), (768, 256)):
-            cols = slice(c0, c0 + width)
-            o = work.tile([P, 4, width], F32, name="o", align_bytes=64)
-            for tp in range(2):
-                m = psum.tile([P, 2, width], F32, name="m2", tag="bank")
-                u = work.tile([P, 2, width], F32, name="u", align_bytes=64)
-                for tl in range(2):
-                    stage2(1, 2 * tp + tl, c0, width, m[:, tl, :])
-                for tl in range(2):
-                    t = 2 * tp + tl
-                    nc.vector.scalar_tensor_tensor(
-                        out=u[:, tl, :], in0=m[:, tl, :], scalar=r2[:, t : t + 1], in1=a[:, t, cols], op0=MUL, op1=ADD
-                    )
-                pend.append((o, tp, u, cols, c0, width))
-                if len(pend) > 1:
-                    step(nc, pend.pop(0), p_b, out_rows, finish)
-                if tp == 1 and late:
-                    quant_out()
-        while pend:
-            step(nc, pend.pop(0), p_b, out_rows, finish)
-        while late:
-            quant_out()
-
-
-def step(nc, item, p_b, out_rows, finish):
-    o, tp, u, cols, c0, width = item
-    nc.vector.tensor_tensor(
-        out=o[:, 2 * tp : 2 * tp + 2, :], in0=u[:], in1=p_b[:, cols].unsqueeze(1).to_broadcast([P, 2, width]), op=MUL
-    )
-    nc.sync.dma_start(out=out_rows[:, 2 * tp : 2 * tp + 2, cols], in_=o[:, 2 * tp : 2 * tp + 2, :])
-    if tp == 1:
-        finish(c0, width, o)
+        for i in range(4):
+            F2(i, 0)
+            F2(i, 1)
+            if i < 2:
+                F3(i, 0, nc.gpsimd)
+                F3(i, 1, nc.gpsimd)
+                F4(i, nc.scalar.copy)
+        F3(2, 0, nc.vector)
+        F3(2, 1, nc.vector)
+        F4(2, nc.scalar.copy)
+        F3(3, 0, nc.vector)
+        F3(3, 1, nc.vector)
+        QO(0)
+        F4(3, nc.vector.tensor_copy)
+        QO(1)
+        store_scales(0, 512)
+        QO(3)
+        QO(2)
+        store_scales(512, 512)

@@ -29,8 +29,7 @@ def tile_channelpreconditionedcsplogvarianceratio_x2_kernel(
     with ExitStack() as ctx:
         keep = ctx.enter_context(tc.tile_pool(name="keep", bufs=1))
         work = ctx.enter_context(tc.tile_pool(name="work", bufs=4))
-        psum = ctx.enter_context(tc.psum_pool(name="psum", bufs=7))
-        vpool = ctx.enter_context(tc.psum_pool(name="vpool", bufs=1))
+        psum = ctx.enter_context(tc.psum_pool(name="psum", bufs=8))
         ctx.enter_context(tc.manual_schedule())
 
         x_hbm = [x.rearrange("(g p j) t -> g p j t", g=2, j=4) for x in (x1, x2)]
@@ -42,11 +41,17 @@ def tile_channelpreconditionedcsplogvarianceratio_x2_kernel(
                 nc.sync.dma_start(out=x_half[:], in_=x_hbm[0][g][:, :, 512 * gt : 512 * gt + 512])
                 xs[0, g, gt] = x_half[:]
 
+        tau_rows = keep.tile([P, 512], BF16, name="tau_rows", align_bytes=64)
+        nc.vector.memset(tau_rows[:], 0.0)
+        for k, t in enumerate((tau1, tau2)):
+            nc.scalar.dma_start(out=tau_rows[2 * k : 2 * k + 2, :], in_=t.rearrange("(g c) -> g c", g=2))
         load_x1(0)
         w_sc = keep.tile([P, NF], U8, name="w_sc", align_bytes=64)
         nc.vector.memset(w_sc[:].bitcast(I32), 0)
         ident = keep.tile([P, P], F32, name="ident", align_bytes=64)
         make_identity(nc, ident[:])
+        ident_bf = keep.tile([P, P], BF16, name="ident_bf", align_bytes=64)
+        make_identity(nc, ident_bf[:])
         for q in range(4):
             nc.sync.dma_start(
                 out=w_sc[32 * q : 32 * q + 8, :].bitcast(I32), in_=w_scales[:, 4 * q : 4 * q + 4, :].bitcast(I32)
@@ -56,10 +61,6 @@ def tile_channelpreconditionedcsplogvarianceratio_x2_kernel(
             nc.sync.dma_start(
                 out=w_sb[:, g, :].bitcast(I32), in_=w_words[g].rearrange("p n t -> p (n t)").bitcast(I32)
             )
-        tau = []
-        for k, t in enumerate((tau1, tau2)):
-            tau.append(keep.tile([P, 2, 4], BF16, name="tau_%d" % k, align_bytes=64))
-            nc.sync.dma_start(out=tau[k][:], in_=t.rearrange("(g p s) -> p g s", g=2, s=4))
         load_x1(1)
         for g in range(2):
             x_whole = keep.tile([P, 4, NT], BF16, name="x_1_%d" % g, align_bytes=64)
@@ -67,29 +68,32 @@ def tile_channelpreconditionedcsplogvarianceratio_x2_kernel(
             for gt in range(2):
                 xs[1, g, gt] = x_whole[:, :, 512 * gt : 512 * gt + 512]
         p_b = keep.tile([P, NC], BF16, name="p_b", align_bytes=64)
-        nc.sync.dma_start(out=p_b[:], in_=p.partition_broadcast(P))
 
+        def LOADP():
+            nc.scalar.dma_start(out=p_b[:], in_=p.partition_broadcast(P))
+
+
+        tau = keep.tile([P, 2, 2, 4], BF16, name="tau", align_bytes=64)
         half_tau = keep.tile([P, 2, 2, 4], F32, name="half_tau", align_bytes=64)
 
-        xc, xt, xtq, yg, yq, zsq, xg, vbank = {}, {}, {}, {}, {}, {}, {}, {}
+        xc, xt, xtq, yg, yq, zsq, xg, vbank, m0_bank, tr_bank, z_bank, r_of, v_of = {}, {}, {}, {}, {}, {}, {}, {}, {}, {}, {}, {}, {}
 
-        def TR(k, g, gt):
-            xt[k, g, gt] = work.tile([P, 2048], BF16, name="xt", align_bytes=64)
-            banks = []
-            for jj in range(2):
-                bank = psum.tile([P, 2, 2, P], F32, name="bank")
-                banks.append(bank)
-                for u in range(2):
-                    for jl in range(2):
-                        words = xs[k, g, gt][:, 2 * jj + jl, :].bitcast(F32)
-                        nc.tensor.transpose(
-                            bank[:, u, jl, :], words[:, u:256:2], ident[:]
-                        )
-            for jj in range(2):
-                dst = xt[k, g, gt][:].bitcast(F32).rearrange("p (q j u) -> p q j u", j=4, u=2)
-                nc.scalar.copy(
-                    out=dst[:, :, 2 * jj : 2 * jj + 2, :], in_=banks[jj][:].rearrange("p u j q -> p q j u")
-                )
+        def TR(k, g, gt, jj):
+            bank = psum.tile([P, 2, 2, P], F32, name="bank")
+            tr_bank[k, g, gt, jj] = bank
+            for u in range(2):
+                for jl in range(2):
+                    words = xs[k, g, gt][:, 2 * jj + jl, :].bitcast(F32)
+                    nc.tensor.transpose(bank[:, u, jl, :], words[:, u:256:2], ident[:])
+
+        def C(k, g, gt, jj):
+            if (k, g, gt) not in xt:
+                xt[k, g, gt] = work.tile([P, 2048], BF16, name="xt", align_bytes=64)
+            dst = xt[k, g, gt][:].bitcast(F32).rearrange("p (q j u) -> p q j u", j=4, u=2)
+            nc.scalar.copy(
+                out=dst[:, :, 2 * jj : 2 * jj + 2, :],
+                in_=tr_bank[k, g, gt, jj][:].rearrange("p u j q -> p q j u"),
+            )
 
         def A(k, g, gt):
             xg[k, g, gt] = work.tile([P, 2048], BF16, name="xg", bufs=3, align_bytes=64)
@@ -112,6 +116,21 @@ def tile_channelpreconditionedcsplogvarianceratio_x2_kernel(
             nc.vector.quantize_mx(out=codes[:].bitcast(FP8X4), scales=scales[:], in_=src[:])
             return codes, scales
 
+        tau_bank = []
+
+        def TAU():
+            bank = psum.tile([P, 4, P], BF16, name="tb", tag="bank")
+            for s in range(4):
+                nc.tensor.transpose(bank[:, s, :], tau_rows[:, s:512:4], ident_bf[:])
+            tau_bank.append(bank)
+
+        def HALF():
+            nc.vector.tensor_copy(
+                out=tau[:].rearrange("p k g s -> p (k g) s"), in_=tau_bank[0][:, :, 0:4].rearrange("p s r -> p r s")
+            )
+            for k in range(2):
+                nc.vector.tensor_scalar(out=half_tau[:, k], in0=tau[:, k], scalar1=0.5 - k, scalar2=None, op0=MUL)
+
         def QC(k, g, gt):
             xc[k, g, gt] = quant(xg[k, g, gt], "xc_%d%d%d" % (k, g, gt))
 
@@ -122,11 +141,8 @@ def tile_channelpreconditionedcsplogvarianceratio_x2_kernel(
             yq[k, gt] = quant(yg[k, gt], "yq_%d%d" % (k, gt))
 
         def Z(k, gt, jf):
-            if (gt, jf) == (0, 0):
-                zsq[k] = work.tile([P, 2, 4, 4, P], F32, name="zsq", bufs=2, align_bytes=64)
-            if jf == 0:
-                yg[k, gt] = work.tile([P, 2048], BF16, name="yg", align_bytes=64)
             z = psum.tile([P, 4, P], F32, name="z", tag="bank")
+            z_bank[k, gt, jf] = z
             for s in range(4):
                 for g in range(2):
                     codes, scales = xc[k, g, gt]
@@ -139,49 +155,65 @@ def tile_channelpreconditionedcsplogvarianceratio_x2_kernel(
                         start=(g == 0),
                         stop=(g == 1),
                     )
-            dst = yg[k, gt][:].rearrange("p (t m s) -> p t m s", t=4, s=4)[:, :, 32 * jf : 32 * jf + 32, :]
+
+        def D(k, gt, jf):
+            if (k, gt) not in yg:
+                yg[k, gt] = work.tile([P, 2048], BF16, name="yg", align_bytes=64)
             nc.vector.tensor_tensor(
-                out=dst,
-                in0=z[:].rearrange("p s (m t) -> p t m s", t=4),
-                in1=tau[k][:, gt, :].unsqueeze(1).unsqueeze(1).to_broadcast([P, 4, 32, 4]),
+                out=yg[k, gt][:].rearrange("p (t m s) -> p t m s", t=4, s=4)[:, :, 32 * jf : 32 * jf + 32, :],
+                in0=z_bank[k, gt, jf][:].rearrange("p s (m t) -> p t m s", t=4),
+                in1=tau[:, k, gt, :].unsqueeze(1).unsqueeze(1).to_broadcast([P, 4, 32, 4]),
                 op=MUL,
             )
+
+        def E(k, gt, jf):
+            if k not in zsq:
+                zsq[k] = work.tile([P, 2, 4, 4, P], F32, name="zsq", bufs=2, align_bytes=64)
             nc.scalar.activation(
                 out=zsq[k][:, gt, :, :, 32 * jf : 32 * jf + 32],
-                in_=z[:].rearrange("p s (m t) -> p t s m", t=4),
+                in_=z_bank[k, gt, jf][:].rearrange("p s (m t) -> p t s m", t=4),
                 func=SQUARE,
             )
 
-        def WT(k, gt, engine):
-            for s in range(4):
+        def WT(k, gt, engine, s):
+            if True:
                 sq = zsq[k][:, gt, :, s, :]
                 weight = half_tau[:, k, gt, s : s + 1]
-                if engine == "VS" and s < 2:
+                if engine == "S":
                     nc.scalar.activation(out=sq, in_=sq, func=COPY, scale=weight)
                 elif engine == "G":
                     nc.gpsimd.tensor_scalar(out=sq, in0=sq, scalar1=weight, scalar2=0.0, op0=MUL, op1=ADD)
                 else:
                     nc.vector.tensor_scalar(out=sq, in0=sq, scalar1=weight, scalar2=None, op0=MUL)
 
-        def VAR(k):
-            vbank[k] = vpool.tile([P, 4, P], F32, name="v")
-            for t in range(4):
-                for i in range(8):
+        def VAR(k, groups, tiles):
+            if (k, groups) not in vbank:
+                vbank[k, groups] = psum.tile([P, 4, P], F32, name="v", tag="bank")
+            pieces = [(gt, s) for gt in groups for s in range(4)]
+            for t in tiles:
+                for gt, s in pieces:
                     nc.tensor.matmul(
-                        vbank[k][:, t, :],
-                        zsq[k][:, i // 4, t, i % 4, :],
+                        vbank[k, groups][:, t, :],
+                        zsq[k][:, gt, t, s, :],
                         ident[:],
                         is_transpose=True,
-                        start=(i == 0),
-                        stop=(i == 7),
+                        start=((gt, s) == pieces[0]),
+                        stop=((gt, s) == pieces[-1]),
                     )
 
+        def SUM(k, groups):
+            v = keep.tile([P, 4], F32, name="v_%d_%d" % (k, groups[0]))
+            nc.vector.tensor_reduce(out=v[:], in_=vbank[k, groups][:], op=ADD, axis=mybir.AxisListType.X)
+            if k in v_of:
+                total = keep.tile([P, 4], F32, name="vt_%d" % k)
+                nc.vector.tensor_tensor(out=total[:], in0=v_of[k][:], in1=v[:], op=ADD)
+                v = total
+            v_of[k] = v
+
         def R(k):
-            v = keep.tile([P, 4], F32, name="v_%d" % k)
-            nc.vector.tensor_reduce(out=v[:], in_=vbank[k][:], op=ADD, axis=mybir.AxisListType.X)
             r = keep.tile([P, 4], F32, name="r_%d" % k)
-            nc.vector.reciprocal(out=r[:], in_=v[:])
-            return r
+            nc.vector.reciprocal(out=r[:], in_=v_of[k][:])
+            r_of[k] = r
 
         def stage2(k, t, c0, width, out):
             for gt in range(2):
@@ -197,90 +229,50 @@ def tile_channelpreconditionedcsplogvarianceratio_x2_kernel(
                     stop=(gt == 1),
                 )
 
+        warm = keep.tile([P, 640], BF16, name="warm", align_bytes=64)
+        nc.gpsimd.memset(warm[:], 0.0)
+
+        def WARM(n):
+            for i in range(n):
+                bank = psum.tile([P, 512], F32, name="wb", tag="bank")
+                nc.tensor.matmul(bank[:], warm[:, 0:128], warm[:, 128:640], start=True, stop=True)
+
         a = keep.tile([P, 4, NC], F32, name="a", align_bytes=64)
 
-        def M0(h, r):
-            for t in range(4):
-                m = psum.tile([P, 512], F32, name="m", tag="bank")
-                stage2(0, t, 512 * h, 512, m[:])
-                nc.scalar.activation(out=a[:, t, 512 * h : 512 * h + 512], in_=m[:], func=COPY, scale=r[:, t : t + 1])
+        def M0(h, *tiles):
+            for t in tiles:
+                m0_bank[h, t] = psum.tile([P, 512], F32, name="m", tag="bank")
+                stage2(0, t, 512 * h, 512, m0_bank[h, t][:])
 
-        TR(0, 0, 0)
-        A(0, 0, 0)
-        TR(0, 1, 0)
-        A(0, 1, 0)
-        QC(0, 0, 0)
-        QC(0, 1, 0)
-        A(0, 0, 1)
-        A(0, 1, 1)
-        nc.vector.tensor_scalar(out=half_tau[:, 0], in0=tau[0][:], scalar1=0.5, scalar2=None, op0=MUL)
-        nc.vector.tensor_scalar(out=half_tau[:, 1], in0=tau[1][:], scalar1=-0.5, scalar2=None, op0=MUL)
-        for jf in range(4):
-            Z(0, 0, jf)
-        WT(0, 0, "G")
-        QC(0, 0, 1)
-        QC(0, 1, 1)
-        QT(0, 0, 0)
-        QY(0, 0)
-        TR(0, 0, 1)
-        TR(0, 1, 1)
-        for jf in range(4):
-            Z(0, 1, jf)
-        QT(0, 1, 0)
-        QY(0, 1)
-        WT(0, 1, "V")
-        TR(1, 0, 0)
-        TR(1, 0, 1)
-        VAR(0)
-        QT(0, 0, 1)
-        QT(0, 1, 1)
-        A(1, 0, 0)
-        r1 = R(0)
-        A(1, 1, 0)
-        A(1, 0, 1)
-        M0(0, r1)
-        TR(1, 1, 0)
-        TR(1, 1, 1)
-        QC(1, 0, 0)
-        QC(1, 1, 0)
-        A(1, 1, 1)
-        QT(1, 0, 0)
-        for jf in range(4):
-            Z(1, 0, jf)
-        QC(1, 0, 1)
-        QC(1, 1, 1)
-        QY(1, 0)
-        for jf in range(4):
-            Z(1, 1, jf)
-        WT(1, 0, "G")
-        QY(1, 1)
-        QT(1, 0, 1)
-        WT(1, 1, "VS")
-        M0(1, r1)
-        VAR(1)
-        QT(1, 1, 0)
-        QT(1, 1, 1)
-        r2 = R(1)
+        def F1(h, *tiles):
+            for t in tiles:
+                nc.scalar.activation(
+                    out=a[:, t, 512 * h : 512 * h + 512], in_=m0_bank[h, t][:], func=COPY, scale=r_of[0][:, t : t + 1]
+                )
 
         out_rows = out_0.rearrange("(p t) c -> p t c", t=4)
         words_hbm = out_1[0].rearrange("p m t -> p (m t)").bitcast(I32)
         o_codes = keep.tile([P, NC], U32, name="o_codes", align_bytes=64)
         o_scales = keep.tile([P, NC], U8, name="o_scales", align_bytes=64)
         chunks = [(256 * i, 256) for i in range(4)]
-        u_of, o_of, og_of = {}, {}, {}
+        u_of, o_of, og_of, m2_bank = {}, {}, {}, {}
+
+        def M2(i, tp):
+            c0, width = chunks[i]
+            m2_bank[i, tp] = psum.tile([P, 2, width], F32, name="m2", tag="bank")
+            for tl in range(2):
+                stage2(1, 2 * tp + tl, c0, width, m2_bank[i, tp][:, tl, :])
 
         def F2(i, tp):
             c0, width = chunks[i]
-            m = psum.tile([P, 2, width], F32, name="m2", tag="bank")
-            for tl in range(2):
-                stage2(1, 2 * tp + tl, c0, width, m[:, tl, :])
+            m = m2_bank[i, tp]
             u = work.tile([P, 2, width], F32, name="u", bufs=6, align_bytes=64)
             for tl in range(2):
                 t = 2 * tp + tl
                 nc.vector.scalar_tensor_tensor(
                     out=u[:, tl, :],
                     in0=m[:, tl, :],
-                    scalar=r2[:, t : t + 1],
+                    scalar=r_of[1][:, t : t + 1],
                     in1=a[:, t, c0 : c0 + width],
                     op0=MUL,
                     op1=ADD,
@@ -320,22 +312,203 @@ def tile_channelpreconditionedcsplogvarianceratio_x2_kernel(
                     in_=o_scales[32 * q : 32 * q + 4, cols].bitcast(I32),
                 )
 
-        for i in range(4):
-            F2(i, 0)
-            F2(i, 1)
-            if i < 2:
-                F3(i, 0, nc.gpsimd)
-                F3(i, 1, nc.gpsimd)
-                F4(i, nc.scalar.copy)
+        A(0, 0, 0)
+        TR(0, 0, 0, 1)
+        C(0, 0, 0, 1)
+        TR(0, 0, 0, 0)
+        TR(0, 1, 0, 1)
+        TR(0, 1, 0, 0)
+        A(0, 1, 0)
+        C(0, 1, 0, 0)
+        QC(0, 0, 0)
+        WARM(1)
+        WARM(1)
+        QC(0, 1, 0)
+        TAU()
+        Z(0, 0, 0)
+        A(0, 1, 1)
+        Z(0, 0, 1)
+        C(0, 0, 0, 0)
+        C(0, 1, 0, 1)
+        QT(0, 0, 0)
+        QT(0, 1, 0)
+        TR(0, 1, 1, 0)
+        A(0, 0, 1)
+        HALF()
+        Z(0, 0, 3)
+        Z(0, 0, 2)
+        D(0, 0, 1)
+        WARM(1)
+        E(0, 0, 1)
+        D(0, 0, 0)
+        D(0, 0, 3)
+        E(0, 0, 3)
+        TR(0, 0, 1, 1)
+        QC(0, 0, 1)
+        TR(0, 0, 1, 0)
+        QC(0, 1, 1)
+        E(0, 0, 0)
+        C(0, 1, 1, 0)
+        LOADP()
+        Z(0, 1, 0)
+        C(0, 0, 1, 0)
+        TR(1, 0, 0, 1)
+        C(0, 0, 1, 1)
+        D(0, 0, 2)
+        E(0, 0, 2)
+        A(1, 0, 0)
+        WT(0, 0, "G", 2)
+        A(1, 1, 0)
+        D(0, 1, 0)
+        TR(0, 1, 1, 1)
+        Z(0, 1, 1)
+        D(0, 1, 1)
+        QC(1, 0, 0)
+        WT(0, 0, "G", 1)
+        Z(0, 1, 2)
+        D(0, 1, 2)
+        C(0, 1, 1, 1)
+        E(0, 1, 0)
+        TR(1, 0, 0, 0)
+        C(1, 0, 0, 1)
+        C(1, 0, 0, 0)
+        TR(1, 1, 0, 0)
+        E(0, 1, 1)
+        Z(0, 1, 3)
+        D(0, 1, 3)
+        QC(1, 1, 0)
+        E(0, 1, 2)
+        E(0, 1, 3)
+        WT(0, 1, "V", 1)
+        WARM(1)
+        QY(0, 0)
+        TR(1, 1, 0, 1)
+        TR(1, 0, 1, 0)
+        TR(1, 1, 1, 0)
+        QT(0, 0, 1)
+        WT(0, 1, "V", 0)
+        C(1, 1, 0, 0)
+        TR(1, 0, 1, 1)
+        TR(1, 1, 1, 1)
+        Z(1, 0, 1)
+        C(1, 1, 0, 1)
+        A(1, 0, 1)
+        QT(0, 1, 1)
+        WT(0, 1, "V", 3)
+        Z(1, 0, 0)
+        C(1, 0, 1, 0)
+        WT(0, 1, "V", 2)
+        WT(0, 0, "G", 3)
+        D(1, 0, 1)
+        C(1, 1, 1, 0)
+        Z(1, 0, 3)
+        WT(0, 0, "G", 0)
+        D(1, 0, 0)
+        VAR(0, (0, 1), (2,))
+        QC(1, 0, 1)
+        E(1, 0, 1)
+        E(1, 0, 0)
+        C(1, 0, 1, 1)
+        VAR(0, (0, 1), (0,))
+        Z(1, 0, 2)
+        D(1, 0, 3)
+        E(1, 0, 3)
+        VAR(0, (0, 1), (1,))
+        A(1, 1, 1)
+        QC(1, 1, 1)
+        D(1, 0, 2)
+        VAR(0, (0, 1), (3,))
+        QY(0, 1)
+        C(1, 1, 1, 1)
+        SUM(0, (0, 1))
+        Z(1, 1, 3)
+        D(1, 1, 3)
+        E(1, 0, 2)
+        R(0)
+        Z(1, 1, 0)
+        D(1, 1, 0)
+        QT(1, 1, 1)
+        E(1, 1, 0)
+        Z(1, 1, 2)
+        D(1, 1, 2)
+        WT(1, 0, "G", 2)
+        E(1, 1, 3)
+        Z(1, 1, 1)
+        D(1, 1, 1)
+        M0(1, 3)
+        QY(1, 0)
+        E(1, 1, 2)
+        WT(1, 0, "G", 0)
+        E(1, 1, 1)
+        M0(1, 0)
+        M0(0, 1)
+        WT(1, 0, "G", 3)
+        M0(1, 1)
+        F1(1, 0)
+        QT(1, 0, 1)
+        WT(1, 0, "G", 1)
+        VAR(1, (0,), (3,))
+        WT(1, 1, "S", 0)
+        F1(0, 1)
+        VAR(1, (0,), (1,))
+        VAR(1, (0,), (2,))
+        VAR(1, (0,), (0,))
+        F1(1, 1)
+        WT(1, 1, "V", 2)
+        WT(1, 1, "V", 1)
+        M0(0, 0)
+        WT(1, 1, "V", 3)
+        QY(1, 1)
+        VAR(1, (1,), (0,))
+        VAR(1, (1,), (2,))
+        VAR(1, (1,), (3,))
+        VAR(1, (1,), (1,))
+        SUM(1, (0,))
+        M0(0, 2)
+        F1(1, 3)
+        QT(1, 0, 0)
+        M0(0, 3)
+        QT(1, 1, 0)
+        F1(0, 2)
+        F1(0, 3)
+        SUM(1, (1,))
+        R(1)
+        M2(0, 1)
+        M2(1, 0)
+        F1(0, 0)
+        F2(0, 1)
+        M2(0, 0)
+        F2(0, 0)
+        M2(3, 0)
+        F2(3, 0)
+        M0(1, 2)
+        F3(0, 1, nc.gpsimd)
+        F2(1, 0)
+        F1(1, 2)
+        M2(1, 1)
+        M2(2, 0)
+        F2(1, 1)
+        F3(0, 0, nc.gpsimd)
+        F4(0, nc.scalar.copy)
+        F3(1, 0, nc.gpsimd)
+        M2(2, 1)
+        M2(3, 1)
+        F2(2, 0)
+        F3(1, 1, nc.gpsimd)
+        F4(1, nc.scalar.copy)
+        F2(2, 1)
+        F2(3, 1)
         F3(2, 0, nc.vector)
-        F3(2, 1, nc.vector)
-        F4(2, nc.scalar.copy)
-        F3(3, 0, nc.vector)
         F3(3, 1, nc.vector)
-        QO(0)
-        F4(3, nc.vector.tensor_copy)
+        F3(2, 1, nc.vector)
+        F3(3, 0, nc.vector)
         QO(1)
+        QO(0)
+        F4(2, nc.scalar.copy)
+        WARM(1)
+        F4(3, nc.vector.tensor_copy)
         store_scales(0, 512)
-        QO(3)
         QO(2)
+        QO(3)
+        WARM(1)
         store_scales(512, 512)

from contextlib import ExitStack

import concourse.mybir as mybir
from concourse.masks import make_identity

F32 = mybir.dt.float32
BF16 = mybir.dt.bfloat16
U32 = mybir.dt.uint32
I32 = mybir.dt.int32
U8 = mybir.dt.uint8
FP8X4 = mybir.dt.float8_e4m3fn_x4
MUL = mybir.AluOpType.mult
ADD = mybir.AluOpType.add
COPY = mybir.ActivationFunctionType.Copy
SQUARE = mybir.ActivationFunctionType.Square

P = 128
NF, NC, NT = 512, 1024, 1024
FLOPS = 4 * 2 * NF * NC * NT

SCALAR_A = ((0, 0, 1), (1, 0, 1))
GPSIMD_A = ((0, 1, 1), (1, 1, 1))


def tile_channelpreconditionedcsplogvarianceratio_x2_kernel(
    tc, w_words, w_scales, x1, x2, tau1, tau2, p, out_0, out_1, out_2
):
    nc = tc.nc
    with ExitStack() as ctx:
        keep = ctx.enter_context(tc.tile_pool(name="keep", bufs=1))
        work = ctx.enter_context(tc.tile_pool(name="work", bufs=4))
        psum = ctx.enter_context(tc.psum_pool(name="psum", bufs=8))
        ctx.enter_context(tc.manual_schedule())

        x_hbm = [x.rearrange("(g p j) t -> g p j t", g=2, j=4) for x in (x1, x2)]
        xs = {}

        def load_x1(gt):
            for g in range(2):
                x_half = keep.tile([P, 4, 512], BF16, name="x_0_%d_%d" % (g, gt), align_bytes=64)
                nc.sync.dma_start(out=x_half[:], in_=x_hbm[0][g][:, :, 512 * gt : 512 * gt + 512])
                xs[0, g, gt] = x_half[:]

        tau_rows = keep.tile([P, 512], BF16, name="tau_rows", align_bytes=64)
        nc.vector.memset(tau_rows[:], 0.0)
        for k, t in enumerate((tau1, tau2)):
            nc.scalar.dma_start(out=tau_rows[2 * k : 2 * k + 2, :], in_=t.rearrange("(g c) -> g c", g=2))
        load_x1(0)
        w_sc = keep.tile([P, NF], U8, name="w_sc", align_bytes=64)
        nc.vector.memset(w_sc[:].bitcast(I32), 0)
        ident = keep.tile([P, P], F32, name="ident", align_bytes=64)
        make_identity(nc, ident[:])
        ident_bf = keep.tile([P, P], BF16, name="ident_bf", align_bytes=64)
        make_identity(nc, ident_bf[:])
        for q in range(4):
            nc.sync.dma_start(
                out=w_sc[32 * q : 32 * q + 8, :].bitcast(I32), in_=w_scales[:, 4 * q : 4 * q + 4, :].bitcast(I32)
            )
        w_sb = keep.tile([P, 2, NF], U32, name="w_sb", align_bytes=64)
        for g in range(2):
            nc.sync.dma_start(
                out=w_sb[:, g, :].bitcast(I32), in_=w_words[g].rearrange("p n t -> p (n t)").bitcast(I32)
            )
        load_x1(1)
        for g in range(2):
            x_whole = keep.tile([P, 4, NT], BF16, name="x_1_%d" % g, align_bytes=64)
            nc.sync.dma_start(out=x_whole[:], in_=x_hbm[1][g])
            for gt in range(2):
                xs[1, g, gt] = x_whole[:, :, 512 * gt : 512 * gt + 512]
        p_b = keep.tile([P, NC], BF16, name="p_b", align_bytes=64)

        def LOADP():
            nc.scalar.dma_start(out=p_b[:], in_=p.partition_broadcast(P))


        tau = keep.tile([P, 2, 2, 4], BF16, name="tau", align_bytes=64)
        half_tau = keep.tile([P, 2, 2, 4], F32, name="half_tau", align_bytes=64)

        xc, xt, xtq, yg, yq, zsq, xg, vbank, m0_bank, tr_bank, z_bank, r_of, v_of = {}, {}, {}, {}, {}, {}, {}, {}, {}, {}, {}, {}, {}

        def TR(k, g, gt, jj):
            bank = psum.tile([P, 2, 2, P], F32, name="bank")
            tr_bank[k, g, gt, jj] = bank
            for u in range(2):
                for jl in range(2):
                    words = xs[k, g, gt][:, 2 * jj + jl, :].bitcast(F32)
                    nc.tensor.transpose(bank[:, u, jl, :], words[:, u:256:2], ident[:])

        def C(k, g, gt, jj):
            if (k, g, gt) not in xt:
                xt[k, g, gt] = work.tile([P, 2048], BF16, name="xt", align_bytes=64)
            dst = xt[k, g, gt][:].bitcast(F32).rearrange("p (q j u) -> p q j u", j=4, u=2)
            nc.scalar.copy(
                out=dst[:, :, 2 * jj : 2 * jj + 2, :],
                in_=tr_bank[k, g, gt, jj][:].rearrange("p u j q -> p q j u"),
            )

        def A(k, g, gt):
            xg[k, g, gt] = work.tile([P, 2048], BF16, name="xg", bufs=3, align_bytes=64)
            dst = xg[k, g, gt][:].rearrange("p (s m j) -> p s m j", s=4, j=4)
            src = xs[k, g, gt].rearrange("p j (m s) -> p s m j", s=4)
            if (k, g, gt) in SCALAR_A:
                for s in range(4):
                    nc.scalar.copy(out=dst[:, s], in_=src[:, s])
            elif (k, g, gt) in GPSIMD_A:
                for s in range(4):
                    nc.gpsimd.tensor_scalar(
                        out=dst[:, s], in0=src[:, s], scalar1=1.0, scalar2=0.0, op0=MUL, op1=ADD
                    )
            else:
                nc.vector.tensor_copy(out=dst, in_=src)

        def quant(src, name):
            codes = keep.tile([P, 512], U32, name=name, align_bytes=64)
            scales = keep.tile([P, 512], U8, name=name + "s", align_bytes=64)
            nc.vector.quantize_mx(out=codes[:].bitcast(FP8X4), scales=scales[:], in_=src[:])
            return codes, scales

        tau_bank = []

        def TAU():
            bank = psum.tile([P, 4, P], BF16, name="tb", tag="bank")
            for s in range(4):
                nc.tensor.transpose(bank[:, s, :], tau_rows[:, s:512:4], ident_bf[:])
            tau_bank.append(bank)

        def HALF():
            nc.vector.tensor_copy(
                out=tau[:].rearrange("p k g s -> p (k g) s"), in_=tau_bank[0][:, :, 0:4].rearrange("p s r -> p r s")
            )
            for k in range(2):
                nc.vector.tensor_scalar(out=half_tau[:, k], in0=tau[:, k], scalar1=0.5 - k, scalar2=None, op0=MUL)

        def QC(k, g, gt):
            xc[k, g, gt] = quant(xg[k, g, gt], "xc_%d%d%d" % (k, g, gt))

        def QT(k, g, gt):
            xtq[k, g, gt] = quant(xt[k, g, gt], "xq_%d%d%d" % (k, g, gt))

        def QY(k, gt):
            yq[k, gt] = quant(yg[k, gt], "yq_%d%d" % (k, gt))

        def Z(k, gt, jf):
            z = psum.tile([P, 4, P], F32, name="z", tag="bank")
            z_bank[k, gt, jf] = z
            for s in range(4):
                for g in range(2):
                    codes, scales = xc[k, g, gt]
                    nc.tensor.matmul_mx(
                        out=z[:, s, :],
                        lhsT=codes[:, 128 * s : 128 * s + 128].bitcast(FP8X4),
                        lhsT_scale=scales[:, 128 * s : 128 * s + 128],
                        rhs=w_sb[:, g, 128 * jf : 128 * jf + 128].bitcast(FP8X4),
                        rhs_scale=w_sc[4 * g : P, 128 * jf : 128 * jf + 128],
                        start=(g == 0),
                        stop=(g == 1),
                    )

        def D(k, gt, jf):
            if (k, gt) not in yg:
                yg[k, gt] = work.tile([P, 2048], BF16, name="yg", align_bytes=64)
            nc.vector.tensor_tensor(
                out=yg[k, gt][:].rearrange("p (t m s) -> p t m s", t=4, s=4)[:, :, 32 * jf : 32 * jf + 32, :],
                in0=z_bank[k, gt, jf][:].rearrange("p s (m t) -> p t m s", t=4),
                in1=tau[:, k, gt, :].unsqueeze(1).unsqueeze(1).to_broadcast([P, 4, 32, 4]),
                op=MUL,
            )

        def E(k, gt, jf):
            if k not in zsq:
                zsq[k] = work.tile([P, 2, 4, 4, P], F32, name="zsq", bufs=2, align_bytes=64)
            nc.scalar.activation(
                out=zsq[k][:, gt, :, :, 32 * jf : 32 * jf + 32],
                in_=z_bank[k, gt, jf][:].rearrange("p s (m t) -> p t s m", t=4),
                func=SQUARE,
            )

        def WT(k, gt, engine, s):
            if True:
                sq = zsq[k][:, gt, :, s, :]
                weight = half_tau[:, k, gt, s : s + 1]
                if engine == "S":
                    nc.scalar.activation(out=sq, in_=sq, func=COPY, scale=weight)
                elif engine == "G":
                    nc.gpsimd.tensor_scalar(out=sq, in0=sq, scalar1=weight, scalar2=0.0, op0=MUL, op1=ADD)
                else:
                    nc.vector.tensor_scalar(out=sq, in0=sq, scalar1=weight, scalar2=None, op0=MUL)

        def VAR(k, groups, tiles):
            if (k, groups) not in vbank:
                vbank[k, groups] = psum.tile([P, 4, P], F32, name="v", tag="bank")
            pieces = [(gt, s) for gt in groups for s in range(4)]
            for t in tiles:
                for gt, s in pieces:
                    nc.tensor.matmul(
                        vbank[k, groups][:, t, :],
                        zsq[k][:, gt, t, s, :],
                        ident[:],
                        is_transpose=True,
                        start=((gt, s) == pieces[0]),
                        stop=((gt, s) == pieces[-1]),
                    )

        def SUM(k, groups):
            v = keep.tile([P, 4], F32, name="v_%d_%d" % (k, groups[0]))
            nc.vector.tensor_reduce(out=v[:], in_=vbank[k, groups][:], op=ADD, axis=mybir.AxisListType.X)
            if k in v_of:
                total = keep.tile([P, 4], F32, name="vt_%d" % k)
                nc.vector.tensor_tensor(out=total[:], in0=v_of[k][:], in1=v[:], op=ADD)
                v = total
            v_of[k] = v

        def R(k):
            r = keep.tile([P, 4], F32, name="r_%d" % k)
            nc.vector.reciprocal(out=r[:], in_=v_of[k][:])
            r_of[k] = r

        def stage2(k, t, c0, width, out):
            for gt in range(2):
                codes, scales = xtq[k, c0 // 512, gt]
                cols = slice(c0 % 512, c0 % 512 + width)
                nc.tensor.matmul_mx(
                    out=out,
                    lhsT=yq[k, gt][0][:, 128 * t : 128 * t + 128].bitcast(FP8X4),
                    lhsT_scale=yq[k, gt][1][:, 128 * t : 128 * t + 128],
                    rhs=codes[:, cols].bitcast(FP8X4),
                    rhs_scale=scales[:, cols],
                    start=(gt == 0),
                    stop=(gt == 1),
                )

        warm = keep.tile([P, 640], BF16, name="warm", align_bytes=64)
        nc.gpsimd.memset(warm[:], 0.0)

        def WARM(n):
            for i in range(n):
                bank = psum.tile([P, 512], F32, name="wb", tag="bank")
                nc.tensor.matmul(bank[:], warm[:, 0:128], warm[:, 128:640], start=True, stop=True)

        a = keep.tile([P, 4, NC], F32, name="a", align_bytes=64)

        def M0(h, *tiles):
            for t in tiles:
                m0_bank[h, t] = psum.tile([P, 512], F32, name="m", tag="bank")
                stage2(0, t, 512 * h, 512, m0_bank[h, t][:])

        def F1(h, *tiles):
            for t in tiles:
                nc.scalar.activation(
                    out=a[:, t, 512 * h : 512 * h + 512], in_=m0_bank[h, t][:], func=COPY, scale=r_of[0][:, t : t + 1]
                )

        out_rows = out_0.rearrange("(p t) c -> p t c", t=4)
        words_hbm = out_1[0].rearrange("p m t -> p (m t)").bitcast(I32)
        o_codes = keep.tile([P, NC], U32, name="o_codes", align_bytes=64)
        o_scales = keep.tile([P, NC], U8, name="o_scales", align_bytes=64)
        chunks = [(256 * i, 256) for i in range(4)]
        u_of, o_of, og_of, m2_bank = {}, {}, {}, {}

        def M2(i, tp):
            c0, width = chunks[i]
            m2_bank[i, tp] = psum.tile([P, 2, width], F32, name="m2", tag="bank")
            for tl in range(2):
                stage2(1, 2 * tp + tl, c0, width, m2_bank[i, tp][:, tl, :])

        def F2(i, tp):
            c0, width = chunks[i]
            m = m2_bank[i, tp]
            u = work.tile([P, 2, width], F32, name="u", bufs=6, align_bytes=64)
            for tl in range(2):
                t = 2 * tp + tl
                nc.vector.scalar_tensor_tensor(
                    out=u[:, tl, :],
                    in0=m[:, tl, :],
                    scalar=r_of[1][:, t : t + 1],
                    in1=a[:, t, c0 : c0 + width],
                    op0=MUL,
                    op1=ADD,
                )
            u_of[i, tp] = u

        def F3(i, tp, engine):
            c0, width = chunks[i]
            cols = slice(c0, c0 + width)
            if i not in o_of:
                o_of[i] = work.tile([P, 4, width], F32, name="o", align_bytes=64)
            rows = slice(2 * tp, 2 * tp + 2)
            engine.tensor_tensor(
                out=o_of[i][:, rows, :],
                in0=u_of[i, tp][:],
                in1=p_b[:, cols].unsqueeze(1).to_broadcast([P, 2, width]),
                op=MUL,
            )
            nc.sync.dma_start(out=out_rows[:, rows, cols], in_=o_of[i][:, rows, :])

        def F4(i, copy):
            width = chunks[i][1]
            og_of[i] = work.tile([P, 4 * width], BF16, name="og", align_bytes=64)
            copy(out=og_of[i][:].rearrange("p (c t) -> p c t", t=4), in_=o_of[i][:].rearrange("p t c -> p c t"))

        def QO(i):
            c0, width = chunks[i]
            cols = slice(c0, c0 + width)
            nc.vector.quantize_mx(out=o_codes[:, cols].bitcast(FP8X4), scales=o_scales[:, cols], in_=og_of[i][:])
            nc.sync.dma_start(out=words_hbm[:, cols], in_=o_codes[:, cols].bitcast(I32))

        def store_scales(c0, width):
            cols = slice(c0, c0 + width)
            for q in range(4):
                (nc.sync if q % 2 == 0 else nc.scalar).dma_start(
                    out=out_2[0][4 * q : 4 * q + 4, cols].bitcast(I32),
                    in_=o_scales[32 * q : 32 * q + 4, cols].bitcast(I32),
                )

        A(0, 0, 0)
        TR(0, 0, 0, 1)
        C(0, 0, 0, 1)
        TR(0, 0, 0, 0)
        TR(0, 1, 0, 1)
        TR(0, 1, 0, 0)
        A(0, 1, 0)
        C(0, 1, 0, 0)
        QC(0, 0, 0)
        WARM(1)
        WARM(1)
        QC(0, 1, 0)
        TAU()
        Z(0, 0, 0)
        A(0, 1, 1)
        Z(0, 0, 1)
        C(0, 0, 0, 0)
        C(0, 1, 0, 1)
        QT(0, 0, 0)
        QT(0, 1, 0)
        TR(0, 1, 1, 0)
        A(0, 0, 1)
        HALF()
        Z(0, 0, 3)
        Z(0, 0, 2)
        D(0, 0, 1)
        WARM(1)
        E(0, 0, 1)
        D(0, 0, 0)
        D(0, 0, 3)
        E(0, 0, 3)
        TR(0, 0, 1, 1)
        QC(0, 0, 1)
        TR(0, 0, 1, 0)
        QC(0, 1, 1)
        E(0, 0, 0)
        C(0, 1, 1, 0)
        LOADP()
        Z(0, 1, 0)
        C(0, 0, 1, 0)
        TR(1, 0, 0, 1)
        C(0, 0, 1, 1)
        D(0, 0, 2)
        E(0, 0, 2)
        A(1, 0, 0)
        WT(0, 0, "G", 2)
        A(1, 1, 0)
        D(0, 1, 0)
        TR(0, 1, 1, 1)
        Z(0, 1, 1)
        D(0, 1, 1)
        QC(1, 0, 0)
        WT(0, 0, "G", 1)
        Z(0, 1, 2)
        D(0, 1, 2)
        C(0, 1, 1, 1)
        E(0, 1, 0)
        TR(1, 0, 0, 0)
        C(1, 0, 0, 1)
        C(1, 0, 0, 0)
        TR(1, 1, 0, 0)
        E(0, 1, 1)
        Z(0, 1, 3)
        D(0, 1, 3)
        QC(1, 1, 0)
        E(0, 1, 2)
        E(0, 1, 3)
        WT(0, 1, "V", 1)
        WARM(1)
        QY(0, 0)
        TR(1, 1, 0, 1)
        TR(1, 0, 1, 0)
        TR(1, 1, 1, 0)
        QT(0, 0, 1)
        WT(0, 1, "V", 0)
        C(1, 1, 0, 0)
        TR(1, 0, 1, 1)
        TR(1, 1, 1, 1)
        Z(1, 0, 1)
        C(1, 1, 0, 1)
        A(1, 0, 1)
        QT(0, 1, 1)
        WT(0, 1, "V", 3)
        Z(1, 0, 0)
        C(1, 0, 1, 0)
        WT(0, 1, "V", 2)
        WT(0, 0, "G", 3)
        D(1, 0, 1)
        C(1, 1, 1, 0)
        Z(1, 0, 3)
        WT(0, 0, "G", 0)
        D(1, 0, 0)
        VAR(0, (0, 1), (2,))
        QC(1, 0, 1)
        E(1, 0, 1)
        E(1, 0, 0)
        C(1, 0, 1, 1)
        VAR(0, (0, 1), (0,))
        Z(1, 0, 2)
        D(1, 0, 3)
        E(1, 0, 3)
        VAR(0, (0, 1), (1,))
        A(1, 1, 1)
        QC(1, 1, 1)
        D(1, 0, 2)
        VAR(0, (0, 1), (3,))
        QY(0, 1)
        C(1, 1, 1, 1)
        SUM(0, (0, 1))
        Z(1, 1, 3)
        D(1, 1, 3)
        E(1, 0, 2)
        R(0)
        Z(1, 1, 0)
        D(1, 1, 0)
        QT(1, 1, 1)
        E(1, 1, 0)
        Z(1, 1, 2)
        D(1, 1, 2)
        WT(1, 0, "G", 2)
        E(1, 1, 3)
        Z(1, 1, 1)
        D(1, 1, 1)
        M0(1, 3)
        QY(1, 0)
        E(1, 1, 2)
        WT(1, 0, "G", 0)
        E(1, 1, 1)
        M0(1, 0)
        M0(0, 1)
        WT(1, 0, "G", 3)
        M0(1, 1)
        F1(1, 0)
        QT(1, 0, 1)
        WT(1, 0, "G", 1)
        VAR(1, (0,), (3,))
        WT(1, 1, "S", 0)
        F1(0, 1)
        VAR(1, (0,), (1,))
        VAR(1, (0,), (2,))
        VAR(1, (0,), (0,))
        F1(1, 1)
        WT(1, 1, "V", 2)
        WT(1, 1, "V", 1)
        M0(0, 0)
        WT(1, 1, "V", 3)
        QY(1, 1)
        VAR(1, (1,), (0,))
        VAR(1, (1,), (2,))
        VAR(1, (1,), (3,))
        VAR(1, (1,), (1,))
        SUM(1, (0,))
        M0(0, 2)
        F1(1, 3)
        QT(1, 0, 0)
        M0(0, 3)
        QT(1, 1, 0)
        F1(0, 2)
        F1(0, 3)
        SUM(1, (1,))
        R(1)
        M2(0, 1)
        M2(1, 0)
        F1(0, 0)
        F2(0, 1)
        M2(0, 0)
        F2(0, 0)
        M2(3, 0)
        F2(3, 0)
        M0(1, 2)
        F3(0, 1, nc.gpsimd)
        F2(1, 0)
        F1(1, 2)
        M2(1, 1)
        M2(2, 0)
        F2(1, 1)
        F3(0, 0, nc.gpsimd)
        F4(0, nc.scalar.copy)
        F3(1, 0, nc.gpsimd)
        M2(2, 1)
        M2(3, 1)
        F2(2, 0)
        F3(1, 1, nc.gpsimd)
        F4(1, nc.scalar.copy)
        F2(2, 1)
        F2(3, 1)
        F3(2, 0, nc.vector)
        F3(3, 1, nc.vector)
        F3(2, 1, nc.vector)
        F3(3, 0, nc.vector)
        QO(1)
        QO(0)
        F4(2, nc.scalar.copy)
        WARM(1)
        F4(3, nc.vector.tensor_copy)
        store_scales(0, 512)
        QO(2)
        QO(3)
        WARM(1)
        store_scales(512, 512)
